import numpy as np
import ml_dtypes


def mxq(x, axis, fmt="e4m3"):
    dtype, down = {"e4m3": (ml_dtypes.float8_e4m3fn, 7), "e5m2": (ml_dtypes.float8_e5m2, 14)}[fmt]
    v = np.moveaxis(np.asarray(x, np.float32).astype(ml_dtypes.bfloat16).astype(np.float64), axis, -1)
    blocks = v.reshape(v.shape[:-1] + (-1, 32))
    amax = np.abs(blocks).max(-1, keepdims=True)
    byte = np.maximum(np.where(amax > 0, np.frexp(amax)[1] - 1 + 127, 0) - down, 1)
    scale = np.exp2(byte - 127.0)
    codes = (blocks / scale).astype(np.float32).astype(dtype).astype(np.float64)
    return np.moveaxis((codes * scale).reshape(v.shape), -1, axis)


WIDE = False


def mx_kscale(k):
    if not WIDE:
        return np.ones(k)
    levels = np.array([10, -10, 5, -5, 0])
    if k % 512:
        return np.exp2(np.random.permutation(np.resize(levels, k // 32))).repeat(32)
    a = np.empty((k // 512, 16))
    for p in range(k // 512):
        a[p, :8] = np.random.permutation(np.resize(levels, 8))
        for g in range(8):
            far = levels[np.abs(levels - a[p, g]) >= 10]
            a[p, g + 8] = far[np.random.randint(len(far))]
    return np.exp2(a.ravel()).repeat(32)


BF16 = ml_dtypes.bfloat16


def bf(x):
    return np.asarray(x, np.float32).astype(BF16)


def f64(x):
    return np.asarray(x).astype(np.float64)


B, T, E, D, H = 2, 512, 128, 1024, 512


def sigmoid(v):
    return 1.0 / (1.0 + np.exp(-v))


def draw0():
    s, r, t = mx_kscale(D), mx_kscale(D), mx_kscale(H)
    speaker = np.random.standard_normal((B, 1, D))
    frames = np.random.standard_normal((B, E, D))
    return {"x": bf(np.random.standard_normal((B, T, D)) * s),
            "e": bf(np.sqrt(0.5) * (speaker + frames) * r),
            "y": bf(np.random.uniform(0.5, 1.5, (B, T, D))),
            "w1": bf(np.random.standard_normal((D, H)) / np.sqrt(D) / s[:, None] * t),
            "we": bf(np.random.standard_normal((D, H)) / np.sqrt(D) / r[:, None]),
            "be": bf(0.5 * np.random.standard_normal(H)),
            "w2": bf(3.0 * np.random.standard_normal((H, D)) / np.sqrt(H) / t[:, None])}


def speaker_embedding(e, we, be):
    a = np.maximum((mxq(f64(e), 2, "e4m3") @ mxq(f64(we), 0, "e4m3")) + f64(be), 0.0)
    return np.mean(a, axis=1)


def core(x, e, y, w1, we, be, w2):
    emb = speaker_embedding(e, we, be)
    h = mxq(f64(x), 2, "e4m3") @ mxq(f64(w1), 0, "e4m3")
    z = h * emb[:, None, :]
    m = sigmoid(mxq(z, 2, "e4m3") @ mxq(f64(w2), 0, "e4m3"))
    return m * f64(y)


def e4m3fn_bytes(y):
    return np.clip(np.asarray(y, np.float64), -448.0, 448.0).astype(np.float32).astype(ml_dtypes.float8_e4m3fn).view(np.uint8)


def e4m3fn_values(b):
    return np.asarray(b, np.uint8).view(ml_dtypes.float8_e4m3fn).astype(np.float64)


def setup_inputs():
    d = draw0()
    x0 = np.asarray(d['x']).astype(np.float64)
    s = (np.max(np.abs(x0), axis=(0, 1), keepdims=True) / 448.0).astype(np.float32)
    out = {}
    for k, v in d.items():
        if k == 'x':
            out['x_bytes'] = e4m3fn_bytes(x0 / s.astype(np.float64))
            out['x_scale'] = s
        else:
            out[k] = v
    return out


def reference(x_bytes, x_scale, e, y, w1, we, be, w2):
    return core(e4m3fn_values(x_bytes) * x_scale.astype(np.float64), e, y, w1, we, be, w2)

@@ -1,0 +1,395 @@
+from contextlib import ExitStack
+
+import concourse.mybir as mybir
+from concourse.masks import make_identity
+
+B, T, E, D, H = 2, 512, 128, 1024, 512
+FLOPS = 2 * (B * T * D * H + B * E * D * H + B * T * H * D)
+
+F32 = mybir.dt.float32
+BF16 = mybir.dt.bfloat16
+U32 = mybir.dt.uint32
+U8 = mybir.dt.uint8
+FP8 = mybir.dt.float8_e4m3fn
+FP8X4 = mybir.dt.float8_e4m3fn_x4
+MULT = mybir.AluOpType.mult
+ACT = mybir.ActivationFunctionType
+
+P = 128
+PACK = 4
+GD = D // (P * PACK)
+TILES = T // P
+NB = 512
+
+
+def tile_speakerbeamenrolmentadaptedmask_kernel(tc, x_bytes, x_scale, e, y, w1, we, be, w2, out):
+    nc = tc.nc
+    with ExitStack() as ctx:
+        keep = ctx.enter_context(tc.tile_pool(name="keep", bufs=1))
+        work = ctx.enter_context(tc.tile_pool(name="work", bufs=8))
+        ps_t = ctx.enter_context(tc.psum_pool(name="ps_t", bufs=2))
+        ps_h = ctx.enter_context(tc.psum_pool(name="ps_h", bufs=2))
+        ps_l = ctx.enter_context(tc.psum_pool(name="ps_l", bufs=4))
+        ctx.enter_context(tc.manual_schedule())
+
+        warm = keep.tile([P, 1], F32, name="warm")
+        nc.vector.memset(warm[:], 0.0)
+        sc = keep.tile([P, D // P], F32, name="sc")
+        nc.sync.dma_start(out=sc[:], in_=x_scale.rearrange("a b (p m) -> p (a b m)", p=P))
+        be_raw = keep.tile([P, PACK], BF16, name="be_raw")
+        nc.scalar.dma_start(out=be_raw[:], in_=be.rearrange("(p t) -> p t", t=PACK))
+        nc.scalar.activation(out=warm[:], in_=warm[:], func=ACT.Sigmoid)
+        ident = keep.tile([P, P], F32, name="ident")
+        make_identity(nc, ident[:])
+
+        def load_w(src, name, split):
+            tiles = []
+            view = src.rearrange("(g p j) n -> g p j n", p=P, j=PACK)
+            width = src.shape[1]
+            for g in range(view.shape[0]):
+                t = keep.tile([P, PACK, width], BF16, name=name + str(g))
+                tiles.append(t)
+            return tiles, view
+
+        we_raw, we_v = load_w(we, "we_raw", 1)
+        w1_raw, w1_v = load_w(w1, "w1_raw", 1)
+        w2_raw, w2_v = load_w(w2, "w2_raw", 1)
+        x8 = [keep.tile([P, TILES, D], U8, name="x8_" + str(b)) for b in range(B)]
+        e_raw = keep.tile([P, B, D], BF16, name="e_raw")
+        y_sb = [keep.tile([P, TILES, D], BF16, name="y_sb" + str(b)) for b in range(B)]
+        x_v = [x_bytes[b].rearrange("(p i) d -> p i d", i=TILES) for b in range(B)]
+        y_v = [y[b].rearrange("(p i) d -> p i d", i=TILES) for b in range(B)]
+        o_v = [out[b].rearrange("(p i) d -> p i d", i=TILES) for b in range(B)]
+
+        nc.sync.dma_start(out=x8[0][:, 0:2, :], in_=x_v[0][:, 0:2, :])
+        nc.sync.dma_start(out=we_raw[0][:], in_=we_v[0])
+        nc.sync.dma_start(out=we_raw[1][:], in_=we_v[1])
+        nc.sync.dma_start(out=e_raw[:], in_=e.rearrange("b p d -> p b d"))
+        nc.sync.dma_start(out=w1_raw[0][:], in_=w1_v[0])
+        nc.sync.dma_start(out=x8[0][:, 2:4, :], in_=x_v[0][:, 2:4, :])
+        nc.sync.dma_start(out=w1_raw[1][:], in_=w1_v[1])
+        nc.sync.dma_start(out=x8[1][:], in_=x_v[1])
+        nc.sync.dma_start(out=w2_raw[0][:], in_=w2_v[0])
+        for b in range(B):
+            nc.sync.dma_start(out=y_sb[b][:], in_=y_v[b])
+
+        we_c = keep.tile([P, GD, H], U32, name="we_c", align_bytes=64)
+        we_s = keep.tile([P, GD, H], U8, name="we_s", align_bytes=64)
+        w1_c = keep.tile([P, GD, H], U32, name="w1_c", align_bytes=64)
+        w1_s = keep.tile([P, GD, H], U8, name="w1_s", align_bytes=64)
+        w2_c = keep.tile([P, D], U32, name="w2_c", align_bytes=64)
+        w2_s = keep.tile([P, D], U8, name="w2_s", align_bytes=64)
+        e_g = keep.tile([P, GD, B * E, PACK], BF16, name="e_g", align_bytes=64)
+        e_c = keep.tile([P, GD, B * E], U32, name="e_c", align_bytes=64)
+        e_s = keep.tile([P, GD, B * E], U8, name="e_s", align_bytes=64)
+        emb = keep.tile([P, B, PACK], F32, name="emb")
+        be_mean = keep.tile([P, PACK], F32, name="be_mean")
+        scale_b = keep.tile([P, P, D // P], F32, name="scale_b")
+
+        def copy(eng, dst, src):
+            if eng == "v":
+                nc.vector.tensor_copy(out=dst, in_=src)
+            else:
+                nc.scalar.copy(out=dst, in_=src)
+
+        def lay_permuted(eng, raw, grouped, lo, hi):
+            copy(
+                eng,
+                grouped[:].rearrange("p (t m j) -> p m j t", t=PACK, j=PACK)[:, lo:hi],
+                raw[:].rearrange("p j (m t) -> p m j t", t=PACK)[:, lo:hi],
+            )
+
+        def lay_plain(eng, raw, grouped, lo, hi):
+            copy(
+                eng,
+                grouped[:].rearrange("p (c i j) -> p c j i", i=4, j=PACK)[:, lo:hi],
+                raw.rearrange("p j (c i) -> p c j i", i=4)[:, lo:hi],
+            )
+
+        def quant(grouped, codes, scales):
+            nc.vector.quantize_mx(out=codes.bitcast(FP8X4), scales=scales, in_=grouped)
+
+        grouped = {}
+
+        def lay(which, g, on_vector=0):
+            t = keep.tile([P, NB * PACK], BF16, name="lay_" + which + str(g), align_bytes=64)
+            grouped[which, g] = t
+            for eng, lo, hi in (("v", 0, on_vector), ("s", on_vector, P)):
+                if hi > lo:
+                    if which == "w2":
+                        lay_plain(eng, w2_raw[0][:, :, g * NB : (g + 1) * NB], t, lo, hi)
+                    else:
+                        lay_permuted(eng, (we_raw if which == "we" else w1_raw)[g], t, lo, hi)
+
+        def quant_w(which, g):
+            t = grouped[which, g][:]
+            if which == "we":
+                quant(t, we_c[:, g, :], we_s[:, g, :])
+            elif which == "w1":
+                quant(t, w1_c[:, g, :], w1_s[:, g, :])
+            else:
+                cols = slice(g * NB, (g + 1) * NB)
+                quant(t, w2_c[:, cols], w2_s[:, cols])
+
+        def scale_spread():
+            for half in range(2):
+                ps = ps_l.tile([P, 4, P], F32, name="lg")
+                for m in range(4):
+                    col = half * 4 + m
+                    nc.tensor.transpose(ps[:, m, :], sc[:, col : col + 1].to_broadcast([P, P]), ident[:])
+                copy(
+                    "s" if half == 0 else "v",
+                    scale_b[:, :, half * 4 : half * 4 + 4],
+                    ps[:].rearrange("p m n -> p n m"),
+                )
+
+        def words_t(src_words, ps):
+            for g in range(GD):
+                for u in range(2):
+                    lo = g * 256 + u
+                    nc.tensor.transpose(ps[:, g, u, :], src_words[:, lo : (g + 1) * 256 : 2], ident[:])
+
+        et = {}
+
+        def e_turn(b):
+            ps = ps_t.tile([P, GD, 2, P], F32, name="tp")
+            et[b] = ps
+            words_t(e_raw[:, b, :].bitcast(F32), ps)
+
+        def e_lay(b):
+            nc.scalar.copy(
+                out=e_g[:, :, b * E : (b + 1) * E, :].bitcast(F32),
+                in_=et[b][:].rearrange("p g u r -> p g r u"),
+            )
+
+        def e_quant():
+            quant(
+                e_g[:].rearrange("p g r k -> p (g r k)"),
+                e_c[:].rearrange("p g r -> p (g r)"),
+                e_s[:].rearrange("p g r -> p (g r)"),
+            )
+
+        def bias_mean():
+            nc.vector.tensor_scalar(out=be_mean[:], in0=be_raw[:], scalar1=1.0 / E, scalar2=None, op0=MULT)
+
+        ep = []
+
+        def embed():
+            for half in range(2):
+                ps = ps_l.tile([P, 2, B * E], F32, name="lg")
+                for tt in range(2):
+                    t = half * 2 + tt
+                    for g in range(GD):
+                        nc.tensor.matmul_mx(
+                            out=ps[:, tt, :],
+                            lhsT=we_c[:, g, t * P : (t + 1) * P].bitcast(FP8X4),
+                            lhsT_scale=we_s[:, g, t * P : (t + 1) * P],
+                            rhs=e_c[:, g, :].bitcast(FP8X4),
+                            rhs_scale=e_s[:, g, :],
+                            start=(g == 0),
+                            stop=(g == GD - 1),
+                        )
+                ep.append(ps)
+
+        def relu():
+            for half in range(2):
+                for tt in range(2):
+                    t = half * 2 + tt
+                    for b in range(B):
+                        junk = work.tile([P, E], F32, name="junk")
+                        nc.scalar.activation(
+                            out=junk[:],
+                            in_=ep[half][:, tt, b * E : (b + 1) * E],
+                            func=ACT.Relu,
+                            bias=be_mean[:, t : t + 1],
+                            scale=1.0 / E,
+                            accum_out=emb[:, b, t : t + 1],
+                        )
+
+        xb, xt, xg, xc, xs, hp, zg, zc, zs, lg, mk, ob = ({} for k in range(12))
+
+        def widen(i):
+            b, r = divmod(i, TILES)
+            xb[i] = work.tile([P, D], BF16, name="xb")
+            nc.vector.tensor_tensor(
+                out=xb[i][:],
+                in0=x8[b][:, r, :].bitcast(FP8),
+                in1=scale_b[:].rearrange("p n m -> p (n m)"),
+                op=MULT,
+            )
+
+        def turn(i):
+            ps = ps_t.tile([P, GD, 2, P], F32, name="tp")
+            xt[i] = ps
+            words_t(xb[i][:].bitcast(F32), ps)
+
+        def lay_x(eng, i):
+            xg[i] = work.tile([P, GD, P, PACK], BF16, name="xg", align_bytes=64)
+            copy(
+                eng,
+                xg[i][:].rearrange("p g r k -> p (g r k)").bitcast(F32).rearrange("p (g r u) -> p g r u", g=GD, u=2),
+                xt[i][:].rearrange("p g u r -> p g r u"),
+            )
+
+        def quant_x(i):
+            xc[i] = work.tile([P, GD, P], U32, name="xc", align_bytes=64)
+            xs[i] = work.tile([P, GD, P], U8, name="xs", align_bytes=64)
+            quant(
+                xg[i][:].rearrange("p g r k -> p (g r k)"),
+                xc[i][:].rearrange("p g r -> p (g r)"),
+                xs[i][:].rearrange("p g r -> p (g r)"),
+            )
+
+        def hidden(i):
+            hp[i] = ps_h.tile([P, PACK, P], F32, name="hp")
+            for t in range(PACK):
+                for g in range(GD):
+                    nc.tensor.matmul_mx(
+                        out=hp[i][:, t, :],
+                        lhsT=w1_c[:, g, t * P : (t + 1) * P].bitcast(FP8X4),
+                        lhsT_scale=w1_s[:, g, t * P : (t + 1) * P],
+                        rhs=xc[i][:, g, :].bitcast(FP8X4),
+                        rhs_scale=xs[i][:, g, :],
+                        start=(g == 0),
+                        stop=(g == GD - 1),
+                    )
+
+        def adapt(i):
+            b = i // TILES
+            zg[i] = work.tile([P, P, PACK], BF16, name="zg", align_bytes=64)
+            nc.vector.tensor_tensor(
+                out=zg[i][:],
+                in0=hp[i][:].rearrange("p t n -> p n t"),
+                in1=emb[:, b, :].unsqueeze(1).to_broadcast([P, P, PACK]),
+                op=MULT,
+            )
+
+        def quant_z(i):
+            zc[i] = work.tile([P, P], U32, name="zc", align_bytes=64)
+            zs[i] = work.tile([P, P], U8, name="zs", align_bytes=64)
+            quant(zg[i][:].rearrange("p n t -> p (n t)"), zc[i][:], zs[i][:])
+
+        def logits(i):
+            lg[i] = []
+            for half in range(2):
+                ps = ps_l.tile([P, NB], F32, name="lg")
+                lg[i].append(ps)
+                cols = slice(half * NB, (half + 1) * NB)
+                nc.tensor.matmul_mx(
+                    out=ps[:],
+                    lhsT=zc[i][:].bitcast(FP8X4),
+                    lhsT_scale=zs[i][:],
+                    rhs=w2_c[:, cols].bitcast(FP8X4),
+                    rhs_scale=w2_s[:, cols],
+                    start=True,
+                    stop=True,
+                )
+
+        def gate(i):
+            mk[i] = work.tile([P, D], F32, name="mk")
+            for half in range(2):
+                cols = slice(half * NB, (half + 1) * NB)
+                nc.scalar.activation(out=mk[i][:, cols], in_=lg[i][half][:], func=ACT.Sigmoid)
+
+        def mask(i, parts=1):
+            b, r = divmod(i, TILES)
+            ob[i] = work.tile([P, D], F32, name="ob")
+            w = D // parts
+            for q in range(parts):
+                cols = slice(q * w, (q + 1) * w)
+                nc.vector.tensor_tensor(out=ob[i][:, cols], in0=mk[i][:, cols], in1=y_sb[b][:, r, cols], op=MULT)
+                nc.sync.dma_start(out=o_v[b][:, r, cols], in_=ob[i][:, cols])
+
+        scale_spread()
+        bias_mean()
+        lay("we", 0, on_vector=64)
+        widen(0)
+        e_turn(0)
+        e_turn(1)
+        lay("we", 1)
+        widen(1)
+        quant_w("we", 0)
+        widen(2)
+        e_lay(0)
+        e_lay(1)
+        turn(0)
+        turn(1)
+        lay("w1", 0)
+        widen(3)
+        e_quant()
+        quant_w("we", 1)
+        widen(4)
+        lay_x("s", 0)
+        lay_x("s", 1)
+        turn(2)
+        turn(3)
+        embed()
+        lay("w1", 1)
+        quant_w("w1", 0)
+        quant_x(0)
+        widen(5)
+        quant_x(1)
+        widen(6)
+        relu()
+        lay_x("s", 2)
+        lay_x("s", 3)
+        quant_w("w1", 1)
+        hidden(0)
+        hidden(1)
+        turn(4)
+        turn(5)
+        widen(7)
+        lay("w2", 0)
+        adapt(0)
+        adapt(1)
+        quant_x(2)
+        hidden(2)
+        quant_z(0)
+        quant_x(3)
+        hidden(3)
+        quant_z(1)
+        adapt(2)
+        adapt(3)
+        lay_x("s", 4)
+        lay_x("s", 5)
+        turn(6)
+        turn(7)
+        lay("w2", 1, on_vector=32)
+        quant_w("w2", 0)
+        quant_x(4)
+        hidden(4)
+        quant_z(2)
+        quant_x(5)
+        hidden(5)
+        quant_z(3)
+        adapt(4)
+        lay_x("s", 6)
+        adapt(5)
+        lay_x("s", 7)
+        quant_w("w2", 1)
+        logits(0)
+        quant_x(6)
+        hidden(6)
+        gate(0)
+        logits(1)
+        quant_x(7)
+        hidden(7)
+        gate(1)
+        quant_z(4)
+        mask(0)
+        adapt(6)
+        quant_z(5)
+        logits(2)
+        gate(2)
+        mask(1)
+        adapt(7)
+        quant_z(6)
+        logits(3)
+        gate(3)
+        mask(2)
+        quant_z(7)
+        for i in range(4, 2 * TILES):
+            logits(i)
+            gate(i)
+            mask(i - 1)
+        mask(2 * TILES - 1, parts=2)

@@ -131,17 +131,16 @@ def tile_speakerbeamenrolmentadaptedmask_kernel(tc, x_bytes, x_scale, e, y, w1, 
                 cols = slice(g * NB, (g + 1) * NB)
                 quant(t, w2_c[:, cols], w2_s[:, cols])
 
-        def scale_spread():
-            for half in range(2):
-                ps = ps_l.tile([P, 4, P], F32, name="lg")
-                for m in range(4):
-                    col = half * 4 + m
-                    nc.tensor.transpose(ps[:, m, :], sc[:, col : col + 1].to_broadcast([P, P]), ident[:])
-                copy(
-                    "s" if half == 0 else "v",
-                    scale_b[:, :, half * 4 : half * 4 + 4],
-                    ps[:].rearrange("p m n -> p n m"),
-                )
+        def scale_spread(half):
+            ps = ps_l.tile([P, 4, P], F32, name="lg")
+            for m in range(4):
+                col = half * 4 + m
+                nc.tensor.transpose(ps[:, m, :], sc[:, col : col + 1].to_broadcast([P, P]), ident[:])
+            copy(
+                "s" if half == 0 else "v",
+                scale_b[:, :, half * 4 : half * 4 + 4],
+                ps[:].rearrange("p m n -> p n m"),
+            )
 
         def words_t(src_words, ps):
             for g in range(GD):
@@ -172,39 +171,37 @@ def tile_speakerbeamenrolmentadaptedmask_kernel(tc, x_bytes, x_scale, e, y, w1, 
         def bias_mean():
             nc.vector.tensor_scalar(out=be_mean[:], in0=be_raw[:], scalar1=1.0 / E, scalar2=None, op0=MULT)
 
-        ep = []
+        ep = {}
 
-        def embed():
-            for half in range(2):
-                ps = ps_l.tile([P, 2, B * E], F32, name="lg")
-                for tt in range(2):
-                    t = half * 2 + tt
-                    for g in range(GD):
-                        nc.tensor.matmul_mx(
-                            out=ps[:, tt, :],
-                            lhsT=we_c[:, g, t * P : (t + 1) * P].bitcast(FP8X4),
-                            lhsT_scale=we_s[:, g, t * P : (t + 1) * P],
-                            rhs=e_c[:, g, :].bitcast(FP8X4),
-                            rhs_scale=e_s[:, g, :],
-                            start=(g == 0),
-                            stop=(g == GD - 1),
-                        )
-                ep.append(ps)
+        def embed(half):
+            ps = ps_l.tile([P, 2, B * E], F32, name="lg")
+            for tt in range(2):
+                t = half * 2 + tt
+                for g in range(GD):
+                    nc.tensor.matmul_mx(
+                        out=ps[:, tt, :],
+                        lhsT=we_c[:, g, t * P : (t + 1) * P].bitcast(FP8X4),
+                        lhsT_scale=we_s[:, g, t * P : (t + 1) * P],
+                        rhs=e_c[:, g, :].bitcast(FP8X4),
+                        rhs_scale=e_s[:, g, :],
+                        start=(g == 0),
+                        stop=(g == GD - 1),
+                    )
+            ep[half] = ps
 
-        def relu():
-            for half in range(2):
-                for tt in range(2):
-                    t = half * 2 + tt
-                    for b in range(B):
-                        junk = work.tile([P, E], F32, name="junk")
-                        nc.scalar.activation(
-                            out=junk[:],
-                            in_=ep[half][:, tt, b * E : (b + 1) * E],
-                            func=ACT.Relu,
-                            bias=be_mean[:, t : t + 1],
-                            scale=1.0 / E,
-                            accum_out=emb[:, b, t : t + 1],
-                        )
+        def relu(half):
+            for tt in range(2):
+                t = half * 2 + tt
+                for b in range(B):
+                    junk = work.tile([P, E], F32, name="junk")
+                    nc.scalar.activation(
+                        out=junk[:],
+                        in_=ep[half][:, tt, b * E : (b + 1) * E],
+                        func=ACT.Relu,
+                        bias=be_mean[:, t : t + 1],
+                        scale=1.0 / E,
+                        accum_out=emb[:, b, t : t + 1],
+                    )
 
         xb, xt, xg, xc, xs, hp, zg, zc, zs, lg, mk, ob = ({} for k in range(12))
 
@@ -291,105 +288,117 @@ def tile_speakerbeamenrolmentadaptedmask_kernel(tc, x_bytes, x_scale, e, y, w1, 
                 cols = slice(half * NB, (half + 1) * NB)
                 nc.scalar.activation(out=mk[i][:, cols], in_=lg[i][half][:], func=ACT.Sigmoid)
 
-        def mask(i, parts=1):
+        def mask(i, widths=(D,)):
             b, r = divmod(i, TILES)
             ob[i] = work.tile([P, D], F32, name="ob")
-            w = D // parts
-            for q in range(parts):
-                cols = slice(q * w, (q + 1) * w)
+            lo = 0
+            for w in widths:
+                cols = slice(lo, lo + w)
+                lo += w
                 nc.vector.tensor_tensor(out=ob[i][:, cols], in0=mk[i][:, cols], in1=y_sb[b][:, r, cols], op=MULT)
                 nc.sync.dma_start(out=o_v[b][:, r, cols], in_=ob[i][:, cols])
 
-        scale_spread()
+        scale_spread(1)
+        scale_spread(0)
         bias_mean()
-        lay("we", 0, on_vector=64)
         widen(0)
-        e_turn(0)
-        e_turn(1)
-        lay("we", 1)
-        widen(1)
-        quant_w("we", 0)
-        widen(2)
-        e_lay(0)
-        e_lay(1)
         turn(0)
-        turn(1)
-        lay("w1", 0)
-        widen(3)
-        e_quant()
-        quant_w("we", 1)
-        widen(4)
+        widen(1)
+        lay("we", 1, on_vector=128)
+        lay("we", 0)
         lay_x("s", 0)
+        quant_x(0)
+        e_turn(0)
+        quant_w("we", 1)
+        widen(2)
+        turn(1)
+        widen(3)
+        e_lay(0)
+        quant_w("we", 0)
+        lay("w1", 0)
+        e_turn(1)
+        e_lay(1)
+        e_quant()
+        embed(1)
         lay_x("s", 1)
+        embed(0)
+        quant_w("w1", 0)
+        widen(4)
+        widen(5)
+        lay("w1", 1)
+        quant_x(1)
+        relu(1)
         turn(2)
         turn(3)
-        embed()
-        lay("w1", 1)
-        quant_w("w1", 0)
-        quant_x(0)
-        widen(5)
-        quant_x(1)
         widen(6)
-        relu()
         lay_x("s", 2)
-        lay_x("s", 3)
-        quant_w("w1", 1)
-        hidden(0)
-        hidden(1)
-        turn(4)
-        turn(5)
-        widen(7)
-        lay("w2", 0)
-        adapt(0)
-        adapt(1)
+        lay("w2", 1, on_vector=48)
         quant_x(2)
-        hidden(2)
-        quant_z(0)
-        quant_x(3)
-        hidden(3)
-        quant_z(1)
-        adapt(2)
-        adapt(3)
+        turn(4)
+        quant_w("w1", 1)
+        lay_x("s", 3)
+        relu(0)
+        turn(5)
+        lay("w2", 0)
         lay_x("s", 4)
-        lay_x("s", 5)
-        turn(6)
-        turn(7)
-        lay("w2", 1, on_vector=32)
-        quant_w("w2", 0)
-        quant_x(4)
-        hidden(4)
-        quant_z(2)
-        quant_x(5)
-        hidden(5)
-        quant_z(3)
-        adapt(4)
-        lay_x("s", 6)
-        adapt(5)
-        lay_x("s", 7)
+        hidden(0)
+        widen(7)
+        hidden(1)
         quant_w("w2", 1)
+        quant_x(3)
+        adapt(0)
+        hidden(2)
+        adapt(1)
+        quant_z(0)
+        quant_z(1)
+        quant_w("w2", 0)
+        adapt(2)
+        lay_x("s", 5)
+        hidden(3)
         logits(0)
-        quant_x(6)
-        hidden(6)
+        quant_x(4)
+        quant_x(5)
+        adapt(3)
+        turn(6)
         gate(0)
+        quant_z(2)
+        lay_x("s", 6)
+        quant_z(3)
         logits(1)
-        quant_x(7)
-        hidden(7)
-        gate(1)
-        quant_z(4)
+        hidden(4)
         mask(0)
+        logits(2)
+        adapt(4)
+        quant_x(6)
+        gate(1)
+        hidden(5)
+        adapt(5)
+        turn(7)
+        mask(1)
+        hidden(6)
+        quant_z(4)
+        gate(2)
+        lay_x("s", 7)
+        logits(3)
+        logits(4)
+        gate(3)
         adapt(6)
         quant_z(5)
-        logits(2)
-        gate(2)
-        mask(1)
-        adapt(7)
-        quant_z(6)
-        logits(3)
-        gate(3)
         mask(2)
+        quant_z(6)
+        gate(4)
+        quant_x(7)
+        logits(5)
+        logits(6)
+        hidden(7)
+        gate(5)
+        mask(3)
+        mask(4)
+        adapt(7)
+        mask(5)
         quant_z(7)
-        for i in range(4, 2 * TILES):
-            logits(i)
-            gate(i)
-            mask(i - 1)
-        mask(2 * TILES - 1, parts=2)
+        logits(7)
+        gate(6)
+        gate(7)
+        mask(6)
+        mask(7, (512, 256, 256))

@@ -33,7 +33,7 @@ def tile_speakerbeamenrolmentadaptedmask_kernel(tc, x_bytes, x_scale, e, y, w1, 
         ctx.enter_context(tc.manual_schedule())
 
         warm = keep.tile([P, 1], F32, name="warm")
-        nc.vector.memset(warm[:], 0.0)
+        nc.gpsimd.memset(warm[:], 0.0)
         sc = keep.tile([P, D // P], F32, name="sc")
         nc.sync.dma_start(out=sc[:], in_=x_scale.rearrange("a b (p m) -> p (a b m)", p=P))
         be_raw = keep.tile([P, PACK], BF16, name="be_raw")
@@ -61,11 +61,11 @@ def tile_speakerbeamenrolmentadaptedmask_kernel(tc, x_bytes, x_scale, e, y, w1, 
         y_v = [y[b].rearrange("(p i) d -> p i d", i=TILES) for b in range(B)]
         o_v = [out[b].rearrange("(p i) d -> p i d", i=TILES) for b in range(B)]
 
-        nc.sync.dma_start(out=x8[0][:, 0:2, :], in_=x_v[0][:, 0:2, :])
         nc.sync.dma_start(out=we_raw[0][:], in_=we_v[0])
+        nc.sync.dma_start(out=x8[0][:, 0:2, :], in_=x_v[0][:, 0:2, :])
         nc.sync.dma_start(out=we_raw[1][:], in_=we_v[1])
-        nc.sync.dma_start(out=e_raw[:], in_=e.rearrange("b p d -> p b d"))
         nc.sync.dma_start(out=w1_raw[0][:], in_=w1_v[0])
+        nc.sync.dma_start(out=e_raw[:], in_=e.rearrange("b p d -> p b d"))
         nc.sync.dma_start(out=x8[0][:, 2:4, :], in_=x_v[0][:, 2:4, :])
         nc.sync.dma_start(out=w1_raw[1][:], in_=w1_v[1])
         nc.sync.dma_start(out=x8[1][:], in_=x_v[1])
@@ -137,7 +137,7 @@ def tile_speakerbeamenrolmentadaptedmask_kernel(tc, x_bytes, x_scale, e, y, w1, 
                 col = half * 4 + m
                 nc.tensor.transpose(ps[:, m, :], sc[:, col : col + 1].to_broadcast([P, P]), ident[:])
             copy(
-                "s" if half == 0 else "v",
+                "s",
                 scale_b[:, :, half * 4 : half * 4 + 4],
                 ps[:].rearrange("p m n -> p n m"),
             )
@@ -169,7 +169,7 @@ def tile_speakerbeamenrolmentadaptedmask_kernel(tc, x_bytes, x_scale, e, y, w1, 
             )
 
         def bias_mean():
-            nc.vector.tensor_scalar(out=be_mean[:], in0=be_raw[:], scalar1=1.0 / E, scalar2=None, op0=MULT)
+            nc.gpsimd.tensor_scalar(out=be_mean[:], in0=be_raw[:], scalar1=1.0 / E, scalar2=None, op0=MULT)
 
         ep = {}
 
@@ -301,104 +301,104 @@ def tile_speakerbeamenrolmentadaptedmask_kernel(tc, x_bytes, x_scale, e, y, w1, 
         scale_spread(1)
         scale_spread(0)
         bias_mean()
+        e_turn(1)
+        lay("we", 0, on_vector=80)
         widen(0)
-        turn(0)
+        lay("we", 1)
         widen(1)
-        lay("we", 1, on_vector=128)
-        lay("we", 0)
-        lay_x("s", 0)
-        quant_x(0)
-        e_turn(0)
+        lay("w1", 0, on_vector=64)
+        e_lay(1)
+        quant_w("we", 0)
         quant_w("we", 1)
         widen(2)
-        turn(1)
+        e_turn(0)
         widen(3)
         e_lay(0)
-        quant_w("we", 0)
-        lay("w1", 0)
-        e_turn(1)
-        e_lay(1)
+        turn(0)
         e_quant()
+        turn(1)
         embed(1)
-        lay_x("s", 1)
+        lay("w1", 1)
         embed(0)
-        quant_w("w1", 0)
         widen(4)
         widen(5)
-        lay("w1", 1)
-        quant_x(1)
+        lay_x("s", 0)
         relu(1)
-        turn(2)
-        turn(3)
-        widen(6)
-        lay_x("s", 2)
-        lay("w2", 1, on_vector=48)
-        quant_x(2)
-        turn(4)
         quant_w("w1", 1)
-        lay_x("s", 3)
+        turn(2)
+        lay_x("s", 1)
+        turn(3)
+        quant_x(0)
+        quant_w("w1", 0)
+        quant_x(1)
         relu(0)
-        turn(5)
-        lay("w2", 0)
-        lay_x("s", 4)
+        lay_x("s", 2)
+        widen(6)
+        quant_x(2)
         hidden(0)
+        adapt(0)
         widen(7)
         hidden(1)
-        quant_w("w2", 1)
-        quant_x(3)
-        adapt(0)
-        hidden(2)
-        adapt(1)
+        lay_x("s", 3)
+        turn(4)
+        lay("w2", 0)
         quant_z(0)
+        lay_x("s", 4)
+        turn(5)
+        adapt(1)
+        lay("w2", 1, on_vector=32)
+        hidden(2)
+        quant_x(3)
         quant_z(1)
-        quant_w("w2", 0)
-        adapt(2)
         lay_x("s", 5)
-        hidden(3)
-        logits(0)
         quant_x(4)
-        quant_x(5)
+        adapt(2)
+        hidden(3)
+        hidden(4)
+        quant_w("w2", 0)
         adapt(3)
         turn(6)
-        gate(0)
+        quant_w("w2", 1)
+        turn(7)
         quant_z(2)
+        quant_x(5)
+        logits(0)
         lay_x("s", 6)
-        quant_z(3)
-        logits(1)
-        hidden(4)
-        mask(0)
-        logits(2)
+        hidden(5)
         adapt(4)
         quant_x(6)
-        gate(1)
-        hidden(5)
-        adapt(5)
-        turn(7)
-        mask(1)
         hidden(6)
-        quant_z(4)
-        gate(2)
+        logits(1)
+        quant_z(3)
         lay_x("s", 7)
-        logits(3)
-        logits(4)
-        gate(3)
+        quant_z(4)
+        quant_x(7)
+        adapt(5)
+        gate(0)
         adapt(6)
+        gate(1)
+        logits(2)
+        mask(0)
+        logits(3)
+        gate(2)
+        gate(3)
         quant_z(5)
-        mask(2)
+        logits(4)
+        mask(1)
+        logits(5)
+        hidden(7)
         quant_z(6)
         gate(4)
-        quant_x(7)
-        logits(5)
-        logits(6)
-        hidden(7)
-        gate(5)
+        mask(2)
         mask(3)
         mask(4)
+        gate(5)
+        logits(6)
         adapt(7)
         mask(5)
         quant_z(7)
-        logits(7)
         gate(6)
-        gate(7)
+        logits(7)
         mask(6)
+        gate(7)
         mask(7, (512, 256, 256))

@@ -61,17 +61,19 @@ def tile_speakerbeamenrolmentadaptedmask_kernel(tc, x_bytes, x_scale, e, y, w1, 
         y_v = [y[b].rearrange("(p i) d -> p i d", i=TILES) for b in range(B)]
         o_v = [out[b].rearrange("(p i) d -> p i d", i=TILES) for b in range(B)]
 
-        nc.sync.dma_start(out=we_raw[0][:], in_=we_v[0])
+        for half in range(2):
+            cols = slice(half * 256, (half + 1) * 256)
+            nc.sync.dma_start(out=we_raw[0][:, :, cols], in_=we_v[0][:, :, cols])
         nc.sync.dma_start(out=x8[0][:, 0:2, :], in_=x_v[0][:, 0:2, :])
-        nc.sync.dma_start(out=we_raw[1][:], in_=we_v[1])
-        nc.sync.dma_start(out=w1_raw[0][:], in_=w1_v[0])
+        nc.sync.dma_start(out=w1_raw[1][:], in_=w1_v[1])
         nc.sync.dma_start(out=e_raw[:], in_=e.rearrange("b p d -> p b d"))
         nc.sync.dma_start(out=x8[0][:, 2:4, :], in_=x_v[0][:, 2:4, :])
-        nc.sync.dma_start(out=w1_raw[1][:], in_=w1_v[1])
+        nc.sync.dma_start(out=we_raw[1][:], in_=we_v[1])
         nc.sync.dma_start(out=x8[1][:], in_=x_v[1])
+        nc.sync.dma_start(out=w1_raw[0][:], in_=w1_v[0])
+        nc.sync.dma_start(out=y_sb[0][:], in_=y_v[0])
         nc.sync.dma_start(out=w2_raw[0][:], in_=w2_v[0])
-        for b in range(B):
-            nc.sync.dma_start(out=y_sb[b][:], in_=y_v[b])
+        nc.sync.dma_start(out=y_sb[1][:], in_=y_v[1])
 
         we_c = keep.tile([P, GD, H], U32, name="we_c", align_bytes=64)
         we_s = keep.tile([P, GD, H], U8, name="we_s", align_bytes=64)
@@ -111,10 +113,11 @@ def tile_speakerbeamenrolmentadaptedmask_kernel(tc, x_bytes, x_scale, e, y, w1, 
 
         grouped = {}
 
-        def lay(which, g, on_vector=0):
+        def lay(which, g, on_vector):
+            half = min(64, on_vector) if (which, g) == ("we", 0) else on_vector
             t = keep.tile([P, NB * PACK], BF16, name="lay_" + which + str(g), align_bytes=64)
             grouped[which, g] = t
-            for eng, lo, hi in (("v", 0, on_vector), ("s", on_vector, P)):
+            for eng, lo, hi in (("v", 0, half), ("v", half, on_vector), ("s", on_vector, P)):
                 if hi > lo:
                     if which == "w2":
                         lay_plain(eng, w2_raw[0][:, :, g * NB : (g + 1) * NB], t, lo, hi)
@@ -137,7 +140,7 @@ def tile_speakerbeamenrolmentadaptedmask_kernel(tc, x_bytes, x_scale, e, y, w1, 
                 col = half * 4 + m
                 nc.tensor.transpose(ps[:, m, :], sc[:, col : col + 1].to_broadcast([P, P]), ident[:])
             copy(
-                "s",
+                "s" if half == 0 else "s",
                 scale_b[:, :, half * 4 : half * 4 + 4],
                 ps[:].rearrange("p m n -> p n m"),
             )
@@ -220,12 +223,11 @@ def tile_speakerbeamenrolmentadaptedmask_kernel(tc, x_bytes, x_scale, e, y, w1, 
             xt[i] = ps
             words_t(xb[i][:].bitcast(F32), ps)
 
-        def lay_x(eng, i):
+        def lay_x(i):
             xg[i] = work.tile([P, GD, P, PACK], BF16, name="xg", align_bytes=64)
-            copy(
-                eng,
-                xg[i][:].rearrange("p g r k -> p (g r k)").bitcast(F32).rearrange("p (g r u) -> p g r u", g=GD, u=2),
-                xt[i][:].rearrange("p g u r -> p g r u"),
+            nc.scalar.copy(
+                out=xg[i][:].rearrange("p g r k -> p (g r k)").bitcast(F32).rearrange("p (g r u) -> p g r u", g=GD, u=2),
+                in_=xt[i][:].rearrange("p g u r -> p g r u"),
             )
 
         def quant_x(i):
@@ -266,139 +268,155 @@ def tile_speakerbeamenrolmentadaptedmask_kernel(tc, x_bytes, x_scale, e, y, w1, 
             zs[i] = work.tile([P, P], U8, name="zs", align_bytes=64)
             quant(zg[i][:].rearrange("p n t -> p (n t)"), zc[i][:], zs[i][:])
 
-        def logits(i):
-            lg[i] = []
-            for half in range(2):
-                ps = ps_l.tile([P, NB], F32, name="lg")
-                lg[i].append(ps)
-                cols = slice(half * NB, (half + 1) * NB)
-                nc.tensor.matmul_mx(
-                    out=ps[:],
-                    lhsT=zc[i][:].bitcast(FP8X4),
-                    lhsT_scale=zs[i][:],
-                    rhs=w2_c[:, cols].bitcast(FP8X4),
-                    rhs_scale=w2_s[:, cols],
-                    start=True,
-                    stop=True,
-                )
+        def logits(i, half):
+            lg[i, half] = ps_l.tile([P, NB], F32, name="lg")
+            cols = slice(half * NB, (half + 1) * NB)
+            nc.tensor.matmul_mx(
+                out=lg[i, half][:],
+                lhsT=zc[i][:].bitcast(FP8X4),
+                lhsT_scale=zs[i][:],
+                rhs=w2_c[:, cols].bitcast(FP8X4),
+                rhs_scale=w2_s[:, cols],
+                start=True,
+                stop=True,
+            )
 
-        def gate(i):
-            mk[i] = work.tile([P, D], F32, name="mk")
-            for half in range(2):
-                cols = slice(half * NB, (half + 1) * NB)
-                nc.scalar.activation(out=mk[i][:, cols], in_=lg[i][half][:], func=ACT.Sigmoid)
+        def gate(i, half):
+            if i not in mk:
+                mk[i] = work.tile([P, D], F32, name="mk")
+                ob[i] = work.tile([P, D], F32, name="ob")
+            cols = slice(half * NB, (half + 1) * NB)
+            nc.scalar.activation(out=mk[i][:, cols], in_=lg[i, half][:], func=ACT.Sigmoid)
 
-        def mask(i, widths=(D,)):
+        def mask(i, lo, hi):
             b, r = divmod(i, TILES)
-            ob[i] = work.tile([P, D], F32, name="ob")
-            lo = 0
-            for w in widths:
-                cols = slice(lo, lo + w)
-                lo += w
-                nc.vector.tensor_tensor(out=ob[i][:, cols], in0=mk[i][:, cols], in1=y_sb[b][:, r, cols], op=MULT)
-                nc.sync.dma_start(out=o_v[b][:, r, cols], in_=ob[i][:, cols])
+            cols = slice(lo, hi)
+            nc.vector.tensor_tensor(out=ob[i][:, cols], in0=mk[i][:, cols], in1=y_sb[b][:, r, cols], op=MULT)
+            nc.sync.dma_start(out=o_v[b][:, r, cols], in_=ob[i][:, cols])
 
         scale_spread(1)
+        lay("we", 0, 96)
         scale_spread(0)
         bias_mean()
+        lay("w1", 1, 0)
         e_turn(1)
-        lay("we", 0, on_vector=80)
-        widen(0)
-        lay("we", 1)
-        widen(1)
-        lay("w1", 0, on_vector=64)
-        e_lay(1)
         quant_w("we", 0)
-        quant_w("we", 1)
-        widen(2)
-        e_turn(0)
-        widen(3)
-        e_lay(0)
+        widen(0)
         turn(0)
-        e_quant()
+        e_lay(1)
+        widen(1)
+        lay_x(0)
         turn(1)
-        embed(1)
-        lay("w1", 1)
-        embed(0)
-        widen(4)
-        widen(5)
-        lay_x("s", 0)
-        relu(1)
-        quant_w("w1", 1)
-        turn(2)
-        lay_x("s", 1)
-        turn(3)
+        widen(2)
+        widen(3)
         quant_x(0)
-        quant_w("w1", 0)
+        widen(4)
+        e_turn(0)
+        lay("we", 1, 0)
+        quant_w("w1", 1)
+        lay_x(1)
+        quant_w("we", 1)
         quant_x(1)
-        relu(0)
-        lay_x("s", 2)
-        widen(6)
-        quant_x(2)
-        hidden(0)
-        adapt(0)
-        widen(7)
-        hidden(1)
-        lay_x("s", 3)
+        turn(2)
+        e_lay(0)
+        turn(3)
+        e_quant()
+        embed(0)
+        lay("w1", 0, 0)
+        embed(1)
+        widen(5)
+        lay_x(2)
+        lay_x(3)
         turn(4)
-        lay("w2", 0)
-        quant_z(0)
-        lay_x("s", 4)
-        turn(5)
-        adapt(1)
-        lay("w2", 1, on_vector=32)
-        hidden(2)
+        widen(6)
+        quant_w("w1", 0)
+        relu(0)
+        relu(1)
+        lay_x(4)
+        quant_x(2)
         quant_x(3)
+        hidden(0)
+        widen(7)
+        adapt(0)
+        hidden(1)
+        adapt(1)
+        lay("w2", 0, 0)
+        hidden(2)
+        hidden(3)
+        quant_z(0)
         quant_z(1)
-        lay_x("s", 5)
+        turn(5)
         quant_x(4)
         adapt(2)
-        hidden(3)
-        hidden(4)
-        quant_w("w2", 0)
+        lay_x(5)
         adapt(3)
         turn(6)
-        quant_w("w2", 1)
-        turn(7)
+        lay_x(6)
+        quant_w("w2", 0)
         quant_z(2)
         quant_x(5)
-        logits(0)
-        lay_x("s", 6)
-        hidden(5)
+        hidden(4)
+        logits(0, 0)
+        lay("w2", 1, 0)
         adapt(4)
         quant_x(6)
-        hidden(6)
-        logits(1)
+        hidden(5)
         quant_z(3)
-        lay_x("s", 7)
-        quant_z(4)
-        quant_x(7)
+        logits(1, 0)
+        hidden(6)
+        gate(0, 0)
         adapt(5)
-        gate(0)
-        adapt(6)
-        gate(1)
-        logits(2)
-        mask(0)
-        logits(3)
-        gate(2)
-        gate(3)
+        quant_z(4)
         quant_z(5)
-        logits(4)
-        mask(1)
-        logits(5)
-        hidden(7)
+        turn(7)
+        adapt(6)
+        quant_w("w2", 1)
+        logits(2, 0)
+        gate(1, 0)
+        gate(2, 0)
+        lay_x(7)
+        mask(0, 0, 512)
         quant_z(6)
-        gate(4)
-        mask(2)
-        mask(3)
-        mask(4)
-        gate(5)
-        logits(6)
+        logits(0, 1)
+        logits(1, 1)
+        mask(1, 0, 512)
+        logits(2, 1)
+        gate(0, 1)
+        gate(1, 1)
+        logits(3, 0)
+        logits(3, 1)
+        gate(2, 1)
+        gate(3, 0)
+        gate(3, 1)
+        mask(2, 0, 512)
+        logits(4, 1)
+        quant_x(7)
+        mask(0, 512, 1024)
+        logits(4, 0)
+        gate(4, 1)
+        mask(1, 512, 1024)
+        gate(4, 0)
+        mask(2, 512, 1024)
+        hidden(7)
+        logits(5, 1)
+        mask(3, 0, D)
+        logits(5, 0)
+        gate(5, 0)
+        mask(4, 0, D)
+        logits(6, 0)
         adapt(7)
-        mask(5)
+        gate(6, 0)
+        gate(5, 1)
+        logits(6, 1)
+        gate(6, 1)
+        mask(5, 0, 512)
         quant_z(7)
-        gate(6)
-        logits(7)
-        mask(6)
-        gate(7)
-        mask(7, (512, 256, 256))
+        logits(7, 0)
+        mask(6, 0, 512)
+        logits(7, 1)
+        gate(7, 0)
+        mask(5, 512, 1024)
+        mask(6, 512, 1024)
+        mask(7, 0, 512)
+        gate(7, 1)
+        mask(7, 512, 1024)

from contextlib import ExitStack

import concourse.mybir as mybir
from concourse.masks import make_identity

B, T, E, D, H = 2, 512, 128, 1024, 512
FLOPS = 2 * (B * T * D * H + B * E * D * H + B * T * H * D)

F32 = mybir.dt.float32
BF16 = mybir.dt.bfloat16
U32 = mybir.dt.uint32
U8 = mybir.dt.uint8
FP8 = mybir.dt.float8_e4m3fn
FP8X4 = mybir.dt.float8_e4m3fn_x4
MULT = mybir.AluOpType.mult
ACT = mybir.ActivationFunctionType

P = 128
PACK = 4
GD = D // (P * PACK)
TILES = T // P
NB = 512


def tile_speakerbeamenrolmentadaptedmask_kernel(tc, x_bytes, x_scale, e, y, w1, we, be, w2, out):
    nc = tc.nc
    with ExitStack() as ctx:
        keep = ctx.enter_context(tc.tile_pool(name="keep", bufs=1))
        work = ctx.enter_context(tc.tile_pool(name="work", bufs=8))
        ps_t = ctx.enter_context(tc.psum_pool(name="ps_t", bufs=2))
        ps_h = ctx.enter_context(tc.psum_pool(name="ps_h", bufs=2))
        ps_l = ctx.enter_context(tc.psum_pool(name="ps_l", bufs=4))
        ctx.enter_context(tc.manual_schedule())

        warm = keep.tile([P, 1], F32, name="warm")
        nc.gpsimd.memset(warm[:], 0.0)
        sc = keep.tile([P, D // P], F32, name="sc")
        nc.sync.dma_start(out=sc[:], in_=x_scale.rearrange("a b (p m) -> p (a b m)", p=P))
        be_raw = keep.tile([P, PACK], BF16, name="be_raw")
        nc.scalar.dma_start(out=be_raw[:], in_=be.rearrange("(p t) -> p t", t=PACK))
        nc.scalar.activation(out=warm[:], in_=warm[:], func=ACT.Sigmoid)
        ident = keep.tile([P, P], F32, name="ident")
        make_identity(nc, ident[:])

        def load_w(src, name, split):
            tiles = []
            view = src.rearrange("(g p j) n -> g p j n", p=P, j=PACK)
            width = src.shape[1]
            for g in range(view.shape[0]):
                t = keep.tile([P, PACK, width], BF16, name=name + str(g))
                tiles.append(t)
            return tiles, view

        we_raw, we_v = load_w(we, "we_raw", 1)
        w1_raw, w1_v = load_w(w1, "w1_raw", 1)
        w2_raw, w2_v = load_w(w2, "w2_raw", 1)
        x8 = [keep.tile([P, TILES, D], U8, name="x8_" + str(b)) for b in range(B)]
        e_raw = keep.tile([P, B, D], BF16, name="e_raw")
        y_sb = [keep.tile([P, TILES, D], BF16, name="y_sb" + str(b)) for b in range(B)]
        x_v = [x_bytes[b].rearrange("(p i) d -> p i d", i=TILES) for b in range(B)]
        y_v = [y[b].rearrange("(p i) d -> p i d", i=TILES) for b in range(B)]
        o_v = [out[b].rearrange("(p i) d -> p i d", i=TILES) for b in range(B)]

        for half in range(2):
            cols = slice(half * 256, (half + 1) * 256)
            nc.sync.dma_start(out=we_raw[0][:, :, cols], in_=we_v[0][:, :, cols])
        nc.sync.dma_start(out=x8[0][:, 0:2, :], in_=x_v[0][:, 0:2, :])
        nc.sync.dma_start(out=w1_raw[1][:], in_=w1_v[1])
        nc.sync.dma_start(out=e_raw[:], in_=e.rearrange("b p d -> p b d"))
        nc.sync.dma_start(out=x8[0][:, 2:4, :], in_=x_v[0][:, 2:4, :])
        nc.sync.dma_start(out=we_raw[1][:], in_=we_v[1])
        nc.sync.dma_start(out=x8[1][:], in_=x_v[1])
        nc.sync.dma_start(out=w1_raw[0][:], in_=w1_v[0])
        nc.sync.dma_start(out=y_sb[0][:], in_=y_v[0])
        nc.sync.dma_start(out=w2_raw[0][:], in_=w2_v[0])
        nc.sync.dma_start(out=y_sb[1][:], in_=y_v[1])

        we_c = keep.tile([P, GD, H], U32, name="we_c", align_bytes=64)
        we_s = keep.tile([P, GD, H], U8, name="we_s", align_bytes=64)
        w1_c = keep.tile([P, GD, H], U32, name="w1_c", align_bytes=64)
        w1_s = keep.tile([P, GD, H], U8, name="w1_s", align_bytes=64)
        w2_c = keep.tile([P, D], U32, name="w2_c", align_bytes=64)
        w2_s = keep.tile([P, D], U8, name="w2_s", align_bytes=64)
        e_g = keep.tile([P, GD, B * E, PACK], BF16, name="e_g", align_bytes=64)
        e_c = keep.tile([P, GD, B * E], U32, name="e_c", align_bytes=64)
        e_s = keep.tile([P, GD, B * E], U8, name="e_s", align_bytes=64)
        emb = keep.tile([P, B, PACK], F32, name="emb")
        be_mean = keep.tile([P, PACK], F32, name="be_mean")
        scale_b = keep.tile([P, P, D // P], F32, name="scale_b")

        def copy(eng, dst, src):
            if eng == "v":
                nc.vector.tensor_copy(out=dst, in_=src)
            else:
                nc.scalar.copy(out=dst, in_=src)

        def lay_permuted(eng, raw, grouped, lo, hi):
            copy(
                eng,
                grouped[:].rearrange("p (t m j) -> p m j t", t=PACK, j=PACK)[:, lo:hi],
                raw[:].rearrange("p j (m t) -> p m j t", t=PACK)[:, lo:hi],
            )

        def lay_plain(eng, raw, grouped, lo, hi):
            copy(
                eng,
                grouped[:].rearrange("p (c i j) -> p c j i", i=4, j=PACK)[:, lo:hi],
                raw.rearrange("p j (c i) -> p c j i", i=4)[:, lo:hi],
            )

        def quant(grouped, codes, scales):
            nc.vector.quantize_mx(out=codes.bitcast(FP8X4), scales=scales, in_=grouped)

        grouped = {}

        def lay(which, g, on_vector):
            half = min(64, on_vector) if (which, g) == ("we", 0) else on_vector
            t = keep.tile([P, NB * PACK], BF16, name="lay_" + which + str(g), align_bytes=64)
            grouped[which, g] = t
            for eng, lo, hi in (("v", 0, half), ("v", half, on_vector), ("s", on_vector, P)):
                if hi > lo:
                    if which == "w2":
                        lay_plain(eng, w2_raw[0][:, :, g * NB : (g + 1) * NB], t, lo, hi)
                    else:
                        lay_permuted(eng, (we_raw if which == "we" else w1_raw)[g], t, lo, hi)

        def quant_w(which, g):
            t = grouped[which, g][:]
            if which == "we":
                quant(t, we_c[:, g, :], we_s[:, g, :])
            elif which == "w1":
                quant(t, w1_c[:, g, :], w1_s[:, g, :])
            else:
                cols = slice(g * NB, (g + 1) * NB)
                quant(t, w2_c[:, cols], w2_s[:, cols])

        def scale_spread(half):
            ps = ps_l.tile([P, 4, P], F32, name="lg")
            for m in range(4):
                col = half * 4 + m
                nc.tensor.transpose(ps[:, m, :], sc[:, col : col + 1].to_broadcast([P, P]), ident[:])
            copy(
                "s" if half == 0 else "s",
                scale_b[:, :, half * 4 : half * 4 + 4],
                ps[:].rearrange("p m n -> p n m"),
            )

        def words_t(src_words, ps):
            for g in range(GD):
                for u in range(2):
                    lo = g * 256 + u
                    nc.tensor.transpose(ps[:, g, u, :], src_words[:, lo : (g + 1) * 256 : 2], ident[:])

        et = {}

        def e_turn(b):
            ps = ps_t.tile([P, GD, 2, P], F32, name="tp")
            et[b] = ps
            words_t(e_raw[:, b, :].bitcast(F32), ps)

        def e_lay(b):
            nc.scalar.copy(
                out=e_g[:, :, b * E : (b + 1) * E, :].bitcast(F32),
                in_=et[b][:].rearrange("p g u r -> p g r u"),
            )

        def e_quant():
            quant(
                e_g[:].rearrange("p g r k -> p (g r k)"),
                e_c[:].rearrange("p g r -> p (g r)"),
                e_s[:].rearrange("p g r -> p (g r)"),
            )

        def bias_mean():
            nc.gpsimd.tensor_scalar(out=be_mean[:], in0=be_raw[:], scalar1=1.0 / E, scalar2=None, op0=MULT)

        ep = {}

        def embed(half):
            ps = ps_l.tile([P, 2, B * E], F32, name="lg")
            for tt in range(2):
                t = half * 2 + tt
                for g in range(GD):
                    nc.tensor.matmul_mx(
                        out=ps[:, tt, :],
                        lhsT=we_c[:, g, t * P : (t + 1) * P].bitcast(FP8X4),
                        lhsT_scale=we_s[:, g, t * P : (t + 1) * P],
                        rhs=e_c[:, g, :].bitcast(FP8X4),
                        rhs_scale=e_s[:, g, :],
                        start=(g == 0),
                        stop=(g == GD - 1),
                    )
            ep[half] = ps

        def relu(half):
            for tt in range(2):
                t = half * 2 + tt
                for b in range(B):
                    junk = work.tile([P, E], F32, name="junk")
                    nc.scalar.activation(
                        out=junk[:],
                        in_=ep[half][:, tt, b * E : (b + 1) * E],
                        func=ACT.Relu,
                        bias=be_mean[:, t : t + 1],
                        scale=1.0 / E,
                        accum_out=emb[:, b, t : t + 1],
                    )

        xb, xt, xg, xc, xs, hp, zg, zc, zs, lg, mk, ob = ({} for k in range(12))

        def widen(i):
            b, r = divmod(i, TILES)
            xb[i] = work.tile([P, D], BF16, name="xb")
            nc.vector.tensor_tensor(
                out=xb[i][:],
                in0=x8[b][:, r, :].bitcast(FP8),
                in1=scale_b[:].rearrange("p n m -> p (n m)"),
                op=MULT,
            )

        def turn(i):
            ps = ps_t.tile([P, GD, 2, P], F32, name="tp")
            xt[i] = ps
            words_t(xb[i][:].bitcast(F32), ps)

        def lay_x(i):
            xg[i] = work.tile([P, GD, P, PACK], BF16, name="xg", align_bytes=64)
            nc.scalar.copy(
                out=xg[i][:].rearrange("p g r k -> p (g r k)").bitcast(F32).rearrange("p (g r u) -> p g r u", g=GD, u=2),
                in_=xt[i][:].rearrange("p g u r -> p g r u"),
            )

        def quant_x(i):
            xc[i] = work.tile([P, GD, P], U32, name="xc", align_bytes=64)
            xs[i] = work.tile([P, GD, P], U8, name="xs", align_bytes=64)
            quant(
                xg[i][:].rearrange("p g r k -> p (g r k)"),
                xc[i][:].rearrange("p g r -> p (g r)"),
                xs[i][:].rearrange("p g r -> p (g r)"),
            )

        def hidden(i):
            hp[i] = ps_h.tile([P, PACK, P], F32, name="hp")
            for t in range(PACK):
                for g in range(GD):
                    nc.tensor.matmul_mx(
                        out=hp[i][:, t, :],
                        lhsT=w1_c[:, g, t * P : (t + 1) * P].bitcast(FP8X4),
                        lhsT_scale=w1_s[:, g, t * P : (t + 1) * P],
                        rhs=xc[i][:, g, :].bitcast(FP8X4),
                        rhs_scale=xs[i][:, g, :],
                        start=(g == 0),
                        stop=(g == GD - 1),
                    )

        def adapt(i):
            b = i // TILES
            zg[i] = work.tile([P, P, PACK], BF16, name="zg", align_bytes=64)
            nc.vector.tensor_tensor(
                out=zg[i][:],
                in0=hp[i][:].rearrange("p t n -> p n t"),
                in1=emb[:, b, :].unsqueeze(1).to_broadcast([P, P, PACK]),
                op=MULT,
            )

        def quant_z(i):
            zc[i] = work.tile([P, P], U32, name="zc", align_bytes=64)
            zs[i] = work.tile([P, P], U8, name="zs", align_bytes=64)
            quant(zg[i][:].rearrange("p n t -> p (n t)"), zc[i][:], zs[i][:])

        def logits(i, half):
            lg[i, half] = ps_l.tile([P, NB], F32, name="lg")
            cols = slice(half * NB, (half + 1) * NB)
            nc.tensor.matmul_mx(
                out=lg[i, half][:],
                lhsT=zc[i][:].bitcast(FP8X4),
                lhsT_scale=zs[i][:],
                rhs=w2_c[:, cols].bitcast(FP8X4),
                rhs_scale=w2_s[:, cols],
                start=True,
                stop=True,
            )

        def gate(i, half):
            if i not in mk:
                mk[i] = work.tile([P, D], F32, name="mk")
                ob[i] = work.tile([P, D], F32, name="ob")
            cols = slice(half * NB, (half + 1) * NB)
            nc.scalar.activation(out=mk[i][:, cols], in_=lg[i, half][:], func=ACT.Sigmoid)

        def mask(i, lo, hi):
            b, r = divmod(i, TILES)
            cols = slice(lo, hi)
            nc.vector.tensor_tensor(out=ob[i][:, cols], in0=mk[i][:, cols], in1=y_sb[b][:, r, cols], op=MULT)
            nc.sync.dma_start(out=o_v[b][:, r, cols], in_=ob[i][:, cols])

        scale_spread(1)
        lay("we", 0, 96)
        scale_spread(0)
        bias_mean()
        lay("w1", 1, 0)
        e_turn(1)
        quant_w("we", 0)
        widen(0)
        turn(0)
        e_lay(1)
        widen(1)
        lay_x(0)
        turn(1)
        widen(2)
        widen(3)
        quant_x(0)
        widen(4)
        e_turn(0)
        lay("we", 1, 0)
        quant_w("w1", 1)
        lay_x(1)
        quant_w("we", 1)
        quant_x(1)
        turn(2)
        e_lay(0)
        turn(3)
        e_quant()
        embed(0)
        lay("w1", 0, 0)
        embed(1)
        widen(5)
        lay_x(2)
        lay_x(3)
        turn(4)
        widen(6)
        quant_w("w1", 0)
        relu(0)
        relu(1)
        lay_x(4)
        quant_x(2)
        quant_x(3)
        hidden(0)
        widen(7)
        adapt(0)
        hidden(1)
        adapt(1)
        lay("w2", 0, 0)
        hidden(2)
        hidden(3)
        quant_z(0)
        quant_z(1)
        turn(5)
        quant_x(4)
        adapt(2)
        lay_x(5)
        adapt(3)
        turn(6)
        lay_x(6)
        quant_w("w2", 0)
        quant_z(2)
        quant_x(5)
        hidden(4)
        logits(0, 0)
        lay("w2", 1, 0)
        adapt(4)
        quant_x(6)
        hidden(5)
        quant_z(3)
        logits(1, 0)
        hidden(6)
        gate(0, 0)
        adapt(5)
        quant_z(4)
        quant_z(5)
        turn(7)
        adapt(6)
        quant_w("w2", 1)
        logits(2, 0)
        gate(1, 0)
        gate(2, 0)
        lay_x(7)
        mask(0, 0, 512)
        quant_z(6)
        logits(0, 1)
        logits(1, 1)
        mask(1, 0, 512)
        logits(2, 1)
        gate(0, 1)
        gate(1, 1)
        logits(3, 0)
        logits(3, 1)
        gate(2, 1)
        gate(3, 0)
        gate(3, 1)
        mask(2, 0, 512)
        logits(4, 1)
        quant_x(7)
        mask(0, 512, 1024)
        logits(4, 0)
        gate(4, 1)
        mask(1, 512, 1024)
        gate(4, 0)
        mask(2, 512, 1024)
        hidden(7)
        logits(5, 1)
        mask(3, 0, D)
        logits(5, 0)
        gate(5, 0)
        mask(4, 0, D)
        logits(6, 0)
        adapt(7)
        gate(6, 0)
        gate(5, 1)
        logits(6, 1)
        gate(6, 1)
        mask(5, 0, 512)
        quant_z(7)
        logits(7, 0)
        mask(6, 0, 512)
        logits(7, 1)
        gate(7, 0)
        mask(5, 512, 1024)
        mask(6, 512, 1024)
        mask(7, 0, 512)
        gate(7, 1)
        mask(7, 512, 1024)
